import numpy as np
import ml_dtypes


def mxq(x, axis, fmt="e4m3"):
    dtype, down = {"e4m3": (ml_dtypes.float8_e4m3fn, 7), "e5m2": (ml_dtypes.float8_e5m2, 14)}[fmt]
    v = np.moveaxis(np.asarray(x, np.float32).astype(ml_dtypes.bfloat16).astype(np.float64), axis, -1)
    blocks = v.reshape(v.shape[:-1] + (-1, 32))
    amax = np.abs(blocks).max(-1, keepdims=True)
    byte = np.maximum(np.where(amax > 0, np.frexp(amax)[1] - 1 + 127, 0) - down, 1)
    scale = np.exp2(byte - 127.0)
    codes = (blocks / scale).astype(np.float32).astype(dtype).astype(np.float64)
    return np.moveaxis((codes * scale).reshape(v.shape), -1, axis)


WIDE = False


def mx_kscale(k):
    if not WIDE:
        return np.ones(k)
    levels = np.array([10, -10, 5, -5, 0])
    if k % 512:
        return np.exp2(np.random.permutation(np.resize(levels, k // 32))).repeat(32)
    a = np.empty((k // 512, 16))
    for p in range(k // 512):
        a[p, :8] = np.random.permutation(np.resize(levels, 8))
        for g in range(8):
            far = levels[np.abs(levels - a[p, g]) >= 10]
            a[p, g + 8] = far[np.random.randint(len(far))]
    return np.exp2(a.ravel()).repeat(32)


def f64(x):
    return np.asarray(x).astype(np.float64)


def striped(idx):
    return np.tile(idx.reshape(-1, 16).T, (8, 1)).astype(np.uint16)


def unstriped(offs):
    return offs[:16].T.reshape(-1).astype(np.int64)


def gelu(v):
    return 0.5 * v * (1.0 + np.tanh(np.sqrt(2.0 / np.pi) * (v + 0.044715 * v**3)))


K, T, H, N = 512, 512, 1024, 256


def setup_inputs():
    n = np.random.standard_normal
    s = mx_kscale(K)[:, None]
    u = mx_kscale(H)
    idx = np.random.permutation(H)
    v = np.empty(H)
    v[idx] = u
    return {
        "xT": (n((K, T)) * s).astype(np.float32),
        "w1": (n((K, H)) / np.sqrt(K) / s * v).astype(np.float32),
        "w2": (n((H, N)) / np.sqrt(H) / u[:, None]).astype(np.float32),
        "offs": striped(idx),
    }


def reference(xT, w1, w2, offs):
    idx = unstriped(offs)
    h = gelu(mxq(f64(w1), 0, "e4m3").T @ mxq(f64(xT), 0, "e4m3"))
    return mxq(f64(w2), 0, "e4m3").T @ mxq(h[idx], 0, "e4m3")

@@ -1,0 +1,158 @@
+from contextlib import ExitStack
+
+import concourse.mybir as mybir
+from concourse.masks import make_identity
+
+K, T, H, N = 512, 512, 1024, 256
+FLOPS = 2 * K * H * T + 2 * H * N * T
+
+F32 = mybir.dt.float32
+BF16 = mybir.dt.bfloat16
+U32 = mybir.dt.uint32
+U16 = mybir.dt.uint16
+U8 = mybir.dt.uint8
+FP8X4 = mybir.dt.float8_e4m3fn_x4
+GELU = mybir.ActivationFunctionType.Gelu_apprx_tanh
+MULT, ADD = mybir.AluOpType.mult, mybir.AluOpType.add
+
+P = 128
+PACK = 4
+PAIR = 2 * P
+CHUNK = 256
+PASS = P * PACK
+
+
+def tile_picked_shuffle_mlp_gelu_perm_l_kernel(tc, xT, w1, w2, offs, out):
+    nc = tc.nc
+    with ExitStack() as ctx:
+        keep = ctx.enter_context(tc.tile_pool(name="keep", bufs=1))
+        psum = ctx.enter_context(tc.psum_pool(name="psum", bufs=1))
+
+        pairs = T // PAIR
+        chunks = H // CHUNK
+        passes = H // PASS
+
+        x_rows = xT.rearrange("(p j) t -> p j t", j=PACK)
+        w1_rows = w1.rearrange("(p j) c -> p j c", j=PACK)
+        w2_rows = w2.rearrange("(g p j) m -> g p j m", g=passes, j=PACK)
+
+        x_raw = [keep.tile([P, PACK, PAIR], F32, name=f"x_raw{b}") for b in range(pairs)]
+        w1_raw = [keep.tile([P, PACK, CHUNK], F32, name=f"w1_raw{q}") for q in range(chunks)]
+        w2_raw = [keep.tile([P, PACK, N], F32, name=f"w2_raw{g}") for g in range(passes)]
+        offsets = keep.tile([P, H // 16], U16, name="offsets")
+
+        nc.sync.dma_start(out=x_raw[0][:], in_=x_rows[:, :, 0:PAIR])
+        nc.sync.dma_start(out=w1_raw[0][:], in_=w1_rows[:, :, 0:CHUNK])
+        nc.sync.dma_start(offsets[:], offs)
+        for q in range(1, chunks):
+            nc.sync.dma_start(out=w1_raw[q][:], in_=w1_rows[:, :, q * CHUNK : (q + 1) * CHUNK])
+        for b in range(1, pairs):
+            nc.sync.dma_start(out=x_raw[b][:], in_=x_rows[:, :, b * PAIR : (b + 1) * PAIR])
+        for g in range(passes):
+            nc.sync.dma_start(out=w2_raw[g][:], in_=w2_rows[g])
+
+        ident = keep.tile([P, P], BF16, name="ident")
+        make_identity(nc, ident[:])
+        warm_in = keep.tile([P, 1], F32, name="warm_in")
+        warm_out = keep.tile([P, 1], F32, name="warm_out")
+        nc.vector.memset(warm_in[:], 0.0)
+        nc.scalar.activation(warm_out[:], warm_in[:], GELU)
+
+        def interleave(engine_copy, grouped, raw):
+            engine_copy(out=grouped.rearrange("p (c j) -> p c j", j=PACK), in_=raw.rearrange("p j c -> p c j"))
+
+        def operand(width, name):
+            grouped = keep.tile([P, PACK * width], BF16, name=name + "_grouped", align_bytes=64)
+            codes = keep.tile([P, width], U32, name=name + "_codes", align_bytes=64)
+            scales = keep.tile([P, width], U8, name=name + "_scales", align_bytes=64)
+            return grouped, codes, scales
+
+        def quantize(op, lo, hi):
+            grouped, codes, scales = op
+            nc.vector.quantize_mx(
+                out=codes[:, lo:hi].bitcast(FP8X4), scales=scales[:, lo:hi], in_=grouped[:, PACK * lo : PACK * hi]
+            )
+
+        def multiply(bank, left, l0, right, r0, width, start, stop):
+            nc.tensor.matmul_mx(
+                out=bank,
+                lhsT=left[1][:, l0 : l0 + P].bitcast(FP8X4),
+                lhsT_scale=left[2][:, l0 : l0 + P],
+                rhs=right[1][:, r0 : r0 + width].bitcast(FP8X4),
+                rhs_scale=right[2][:, r0 : r0 + width],
+                start=start,
+                stop=stop,
+            )
+
+        x_op = [operand(PAIR, f"x{b}") for b in range(pairs)]
+        w1_op = [operand(CHUNK, f"w1_{q}") for q in range(chunks)]
+        w2_op = [operand(N, f"w2_{g}") for g in range(passes)]
+        window = [keep.tile([P, 2 * H], BF16, name=f"window{b}", align_bytes=64) for b in range(pairs)]
+
+        def first_layer(b, q):
+            bank = psum.tile([P, 2, CHUNK], F32, name=f"bank{4 * b + q}")
+            for h in range(2):
+                multiply(bank[:, h, :], x_op[b], h * P, w1_op[q], 0, CHUNK, True, True)
+            nc.scalar.activation(
+                window[b][:, 2 * q * CHUNK : 2 * (q + 1) * CHUNK].rearrange("p (c h) -> p c h", h=2),
+                bank[:].rearrange("p h c -> p c h"),
+                GELU,
+            )
+
+        interleave(nc.vector.tensor_copy, x_op[0][0][:], x_raw[0][:])
+        quantize(x_op[0], 0, PAIR)
+        for q in range(chunks):
+            half = CHUNK // 2
+            for s in range(2):
+                interleave(
+                    nc.vector.tensor_copy,
+                    w1_op[q][0][:, PACK * s * half : PACK * (s + 1) * half],
+                    w1_raw[q][:, :, s * half : (s + 1) * half],
+                )
+            for s in range(2):
+                quantize(w1_op[q], s * half, (s + 1) * half)
+            first_layer(0, q)
+        for b in range(1, pairs):
+            interleave(nc.vector.tensor_copy, x_op[b][0][:], x_raw[b][:])
+            quantize(x_op[b], 0, PAIR)
+            for q in range(chunks):
+                first_layer(b, q)
+
+        for g in range(passes):
+            nc.gpsimd.tensor_scalar(
+                out=w2_op[g][0][:].rearrange("p (c j) -> p c j", j=PACK),
+                in0=w2_raw[g][:].rearrange("p j c -> p c j"),
+                scalar1=1.0, scalar2=0.0, op0=MULT, op1=ADD,
+            )
+
+        h_op = [[operand(PAIR, f"h{b}_{g}") for g in range(passes)] for b in range(pairs)]
+        for b in range(pairs):
+            for g in range(passes):
+                picked = keep.tile([P, 2 * PASS], BF16, name=f"picked{b}_{g}", align_bytes=64)
+                cols = PASS // 16
+                nc.vector.tensor_copy(
+                    picked[:].bitcast(U32), window[b][:].bitcast(U32).indirect(offsets[:, g * cols : (g + 1) * cols])
+                )
+                view = picked[:].rearrange("p (q e h) -> p h e q", e=PACK, h=2)
+                for h in range(2):
+                    turned = psum.tile([P, PACK, P], BF16, name=f"bank{4 * b + 2 * g + h}")
+                    for e in range(PACK):
+                        nc.tensor.transpose(turned[:, e, :], view[:, h, e, :], ident[:])
+                    copy = nc.scalar.copy if h == 0 or b == 0 else nc.vector.tensor_copy
+                    copy(
+                        out=h_op[b][g][0][:, h * PASS : (h + 1) * PASS].rearrange("p (t e) -> p t e", e=PACK),
+                        in_=turned[:].rearrange("p e t -> p t e"),
+                    )
+                if b == 0:
+                    quantize(w2_op[g], 0, N)
+                quantize(h_op[b][g], 0, PAIR)
+            for m in range(N // P):
+                bank = psum.tile([P, PAIR], F32, name=f"bank{4 * b + m}")
+                for g in range(passes):
+                    multiply(bank[:], w2_op[g], m * P, h_op[b][g], 0, PAIR, g == 0, g == passes - 1)
+                result = keep.tile([P, PAIR], F32, name=f"result{b}_{m}")
+                if m == 0:
+                    nc.vector.tensor_copy(out=result[:], in_=bank[:])
+                else:
+                    nc.scalar.copy(out=result[:], in_=bank[:])
+                nc.sync.dma_start(out=out[m * P : (m + 1) * P, b * PAIR : (b + 1) * PAIR], in_=result[:])

@@ -51,7 +51,7 @@ def tile_picked_shuffle_mlp_gelu_perm_l_kernel(tc, xT, w1, w2, offs, out):
         for g in range(passes):
             nc.sync.dma_start(out=w2_raw[g][:], in_=w2_rows[g])
 
-        ident = keep.tile([P, P], BF16, name="ident")
+        ident = keep.tile([P, P], F32, name="ident")
         make_identity(nc, ident[:])
         warm_in = keep.tile([P, 1], F32, name="warm_in")
         warm_out = keep.tile([P, 1], F32, name="warm_out")
@@ -131,27 +131,29 @@ def tile_picked_shuffle_mlp_gelu_perm_l_kernel(tc, xT, w1, w2, offs, out):
                 picked = keep.tile([P, 2 * PASS], BF16, name=f"picked{b}_{g}", align_bytes=64)
                 cols = PASS // 16
                 nc.vector.tensor_copy(
-                    picked[:].bitcast(U32), window[b][:].bitcast(U32).indirect(offsets[:, g * cols : (g + 1) * cols])
+                    picked[:].bitcast(U32).rearrange("p (e q) -> p q e", e=PACK),
+                    window[b][:].bitcast(U32).indirect(offsets[:, g * cols : (g + 1) * cols]),
                 )
-                view = picked[:].rearrange("p (q e h) -> p h e q", e=PACK, h=2)
-                for h in range(2):
-                    turned = psum.tile([P, PACK, P], BF16, name=f"bank{4 * b + 2 * g + h}")
-                    for e in range(PACK):
-                        nc.tensor.transpose(turned[:, e, :], view[:, h, e, :], ident[:])
-                    copy = nc.scalar.copy if h == 0 or b == 0 else nc.vector.tensor_copy
-                    copy(
-                        out=h_op[b][g][0][:, h * PASS : (h + 1) * PASS].rearrange("p (t e) -> p t e", e=PACK),
-                        in_=turned[:].rearrange("p e t -> p t e"),
-                    )
+                words = picked[:].bitcast(F32).rearrange("p (e q) -> p e q", e=PACK)
+                turned = psum.tile([P, PACK, P], F32, name=f"bank{4 * b + g}")
+                for e in range(PACK):
+                    nc.tensor.transpose(turned[:, e, :], words[:, e, :], ident[:])
+                source = turned[:].rearrange("p e t -> p (e t)").bitcast(BF16).rearrange("p (e t h) -> p h t e", e=PACK, h=2)
+                target = h_op[b][g][0][:].rearrange("p (h t e) -> p h t e", h=2, e=PACK)
+                if (b, g) == (1, 1):
+                    for h in range(2):
+                        nc.scalar.copy(out=target[:, h], in_=source[:, h])
+                else:
+                    nc.scalar.copy(out=target, in_=source)
                 if b == 0:
                     quantize(w2_op[g], 0, N)
                 quantize(h_op[b][g], 0, PAIR)
             for m in range(N // P):
-                bank = psum.tile([P, PAIR], F32, name=f"bank{4 * b + m}")
+                bank = psum.tile([P, PAIR], F32, name=f"bank{4 * b + 2 + m}")
                 for g in range(passes):
                     multiply(bank[:], w2_op[g], m * P, h_op[b][g], 0, PAIR, g == 0, g == passes - 1)
                 result = keep.tile([P, PAIR], F32, name=f"result{b}_{m}")
-                if m == 0:
+                if m == 0 and b == 1:
                     nc.vector.tensor_copy(out=result[:], in_=bank[:])
                 else:
                     nc.scalar.copy(out=result[:], in_=bank[:])

@@ -37,22 +37,26 @@ def tile_picked_shuffle_mlp_gelu_perm_l_kernel(tc, xT, w1, w2, offs, out):
         w2_rows = w2.rearrange("(g p j) m -> g p j m", g=passes, j=PACK)
 
         x_raw = [keep.tile([P, PACK, PAIR], F32, name=f"x_raw{b}") for b in range(pairs)]
-        w1_raw = [keep.tile([P, PACK, CHUNK], F32, name=f"w1_raw{q}") for q in range(chunks)]
         w2_raw = [keep.tile([P, PACK, N], F32, name=f"w2_raw{g}") for g in range(passes)]
         offsets = keep.tile([P, H // 16], U16, name="offsets")
 
         nc.sync.dma_start(out=x_raw[0][:], in_=x_rows[:, :, 0:PAIR])
-        nc.sync.dma_start(out=w1_raw[0][:], in_=w1_rows[:, :, 0:CHUNK])
-        nc.sync.dma_start(offsets[:], offs)
-        for q in range(1, chunks):
-            nc.sync.dma_start(out=w1_raw[q][:], in_=w1_rows[:, :, q * CHUNK : (q + 1) * CHUNK])
+        w1_raw = []
+        for width in (2 * CHUNK, CHUNK, CHUNK):
+            first = CHUNK * len(w1_raw)
+            part = keep.tile([P, PACK, width], F32, name=f"w1_raw{first}")
+            nc.sync.dma_start(out=part[:], in_=w1_rows[:, :, first : first + width])
+            w1_raw += [part[:, :, s : s + CHUNK] for s in range(0, width, CHUNK)]
         for b in range(1, pairs):
             nc.sync.dma_start(out=x_raw[b][:], in_=x_rows[:, :, b * PAIR : (b + 1) * PAIR])
+        nc.sync.dma_start(offsets[:], offs)
         for g in range(passes):
             nc.sync.dma_start(out=w2_raw[g][:], in_=w2_rows[g])
 
-        ident = keep.tile([P, P], F32, name="ident")
+        ident = keep.tile([P, P], BF16, name="ident")
         make_identity(nc, ident[:])
+        ident_words = keep.tile([P, P], F32, name="ident_words")
+        make_identity(nc, ident_words[:])
         warm_in = keep.tile([P, 1], F32, name="warm_in")
         warm_out = keep.tile([P, 1], F32, name="warm_out")
         nc.vector.memset(warm_in[:], 0.0)
@@ -61,8 +65,8 @@ def tile_picked_shuffle_mlp_gelu_perm_l_kernel(tc, xT, w1, w2, offs, out):
         def interleave(engine_copy, grouped, raw):
             engine_copy(out=grouped.rearrange("p (c j) -> p c j", j=PACK), in_=raw.rearrange("p j c -> p c j"))
 
-        def operand(width, name):
-            grouped = keep.tile([P, PACK * width], BF16, name=name + "_grouped", align_bytes=64)
+        def operand(width, name, tag=None):
+            grouped = keep.tile([P, PACK * width], BF16, name=name + "_grouped", tag=tag or name + "_grouped", align_bytes=64)
             codes = keep.tile([P, width], U32, name=name + "_codes", align_bytes=64)
             scales = keep.tile([P, width], U8, name=name + "_scales", align_bytes=64)
             return grouped, codes, scales
@@ -86,7 +90,6 @@ def tile_picked_shuffle_mlp_gelu_perm_l_kernel(tc, xT, w1, w2, offs, out):
 
         x_op = [operand(PAIR, f"x{b}") for b in range(pairs)]
         w1_op = [operand(CHUNK, f"w1_{q}") for q in range(chunks)]
-        w2_op = [operand(N, f"w2_{g}") for g in range(passes)]
         window = [keep.tile([P, 2 * H], BF16, name=f"window{b}", align_bytes=64) for b in range(pairs)]
 
         def first_layer(b, q):
@@ -105,7 +108,7 @@ def tile_picked_shuffle_mlp_gelu_perm_l_kernel(tc, xT, w1, w2, offs, out):
             half = CHUNK // 2
             for s in range(2):
                 interleave(
-                    nc.vector.tensor_copy,
+                    nc.scalar.copy if (q, s) == (1, 1) else nc.vector.tensor_copy,
                     w1_op[q][0][:, PACK * s * half : PACK * (s + 1) * half],
                     w1_raw[q][:, :, s * half : (s + 1) * half],
                 )
@@ -118,6 +121,7 @@ def tile_picked_shuffle_mlp_gelu_perm_l_kernel(tc, xT, w1, w2, offs, out):
             for q in range(chunks):
                 first_layer(b, q)
 
+        w2_op = [operand(N, "w2_0", "x1_grouped"), operand(N, "w2_1")]
         for g in range(passes):
             nc.gpsimd.tensor_scalar(
                 out=w2_op[g][0][:].rearrange("p (c j) -> p c j", j=PACK),
@@ -126,35 +130,60 @@ def tile_picked_shuffle_mlp_gelu_perm_l_kernel(tc, xT, w1, w2, offs, out):
             )
 
         h_op = [[operand(PAIR, f"h{b}_{g}") for g in range(passes)] for b in range(pairs)]
+        picked = {}
         for b in range(pairs):
             for g in range(passes):
-                picked = keep.tile([P, 2 * PASS], BF16, name=f"picked{b}_{g}", align_bytes=64)
+                picked[b, g] = keep.tile([P, 2 * PASS], BF16, name=f"picked{b}_{g}", align_bytes=64)
                 cols = PASS // 16
                 nc.vector.tensor_copy(
-                    picked[:].bitcast(U32).rearrange("p (e q) -> p q e", e=PACK),
+                    picked[b, g][:].bitcast(U32).rearrange("p (e q) -> p q e", e=PACK),
                     window[b][:].bitcast(U32).indirect(offsets[:, g * cols : (g + 1) * cols]),
                 )
-                words = picked[:].bitcast(F32).rearrange("p (e q) -> p e q", e=PACK)
-                turned = psum.tile([P, PACK, P], F32, name=f"bank{4 * b + g}")
-                for e in range(PACK):
-                    nc.tensor.transpose(turned[:, e, :], words[:, e, :], ident[:])
-                source = turned[:].rearrange("p e t -> p (e t)").bitcast(BF16).rearrange("p (e t h) -> p h t e", e=PACK, h=2)
-                target = h_op[b][g][0][:].rearrange("p (h t e) -> p h t e", h=2, e=PACK)
-                if (b, g) == (1, 1):
-                    for h in range(2):
-                        nc.scalar.copy(out=target[:, h], in_=source[:, h])
-                else:
-                    nc.scalar.copy(out=target, in_=source)
-                if b == 0:
-                    quantize(w2_op[g], 0, N)
-                quantize(h_op[b][g], 0, PAIR)
+
+        def turn(b, g, name):
+            words = picked[b, g][:].bitcast(F32).rearrange("p (e q) -> p e q", e=PACK)
+            turned = psum.tile([P, PACK, P], F32, name=name)
+            for e in range(PACK):
+                nc.tensor.transpose(turned[:, e, :], words[:, e, :], ident_words[:])
+            nc.scalar.copy(
+                out=h_op[b][g][0][:].rearrange("p (h t e) -> p h t e", h=2, e=PACK),
+                in_=turned[:].rearrange("p e t -> p (e t)").bitcast(BF16).rearrange("p (e t h) -> p h t e", e=PACK, h=2),
+            )
+
+        def turn_half(b, g, h, copy, name):
+            values = picked[b, g][:].rearrange("p (e q h) -> p h e q", e=PACK, h=2)
+            turned = psum.tile([P, PACK, P], BF16, name=name)
+            for e in range(PACK):
+                nc.tensor.transpose(turned[:, e, :], values[:, h, e, :], ident[:])
+            copy(
+                out=h_op[b][g][0][:, h * PASS : (h + 1) * PASS].rearrange("p (t e) -> p t e", e=PACK),
+                in_=turned[:].rearrange("p e t -> p t e"),
+            )
+
+        turn(0, 0, "bank0")
+        turn(0, 1, "bank1")
+        turn(1, 0, "bank2")
+        turn_half(1, 1, 0, nc.vector.tensor_copy, "bank3")
+        turn_half(1, 1, 1, nc.scalar.copy, "bank4")
+        quantize(w2_op[0], 0, N)
+        quantize(h_op[0][0], 0, PAIR)
+        quantize(w2_op[1], 0, N)
+        quantize(h_op[0][1], 0, PAIR)
+        quantize(h_op[1][0], 0, PAIR)
+        quantize(h_op[1][1], 0, PAIR)
+        sums0 = psum.tile([P, N // P, PAIR], F32, name="bank5")
+        for m in range(N // P):
+            for g in range(passes):
+                multiply(sums0[:, m, :], w2_op[g], m * P, h_op[0][g], 0, PAIR, g == 0, g == passes - 1)
+        sums1 = [psum.tile([P, PAIR], F32, name=f"bank{6 + m}") for m in range(N // P)]
+        for g in range(passes):
             for m in range(N // P):
-                bank = psum.tile([P, PAIR], F32, name=f"bank{4 * b + 2 + m}")
-                for g in range(passes):
-                    multiply(bank[:], w2_op[g], m * P, h_op[b][g], 0, PAIR, g == 0, g == passes - 1)
-                result = keep.tile([P, PAIR], F32, name=f"result{b}_{m}")
-                if m == 0 and b == 1:
-                    nc.vector.tensor_copy(out=result[:], in_=bank[:])
-                else:
-                    nc.scalar.copy(out=result[:], in_=bank[:])
-                nc.sync.dma_start(out=out[m * P : (m + 1) * P, b * PAIR : (b + 1) * PAIR], in_=result[:])
+                multiply(sums1[m][:], w2_op[g], m * P, h_op[1][g], 0, PAIR, g == 0, g == passes - 1)
+        result0 = keep.tile([P, N // P, PAIR], F32, name="result0")
+        nc.scalar.copy(out=result0[:], in_=sums0[:])
+        nc.sync.dma_start(out=out.rearrange("(m p) t -> p m t", p=P)[:, :, :PAIR], in_=result0[:])
+        for m in range(N // P):
+            result = keep.tile([P, PAIR], F32, name=f"result1_{m}")
+            copy = nc.scalar.copy if m else nc.vector.tensor_copy
+            copy(out=result[:], in_=sums1[m][:])
+            nc.sync.dma_start(out=out[m * P : (m + 1) * P, PAIR:], in_=result[:])

@@ -116,8 +116,14 @@ def tile_picked_shuffle_mlp_gelu_perm_l_kernel(tc, xT, w1, w2, offs, out):
                 quantize(w1_op[q], s * half, (s + 1) * half)
             first_layer(0, q)
         for b in range(1, pairs):
-            interleave(nc.vector.tensor_copy, x_op[b][0][:], x_raw[b][:])
-            quantize(x_op[b], 0, PAIR)
+            for h in range(2):
+                interleave(
+                    nc.vector.tensor_copy,
+                    x_op[b][0][:, PACK * h * P : PACK * (h + 1) * P],
+                    x_raw[b][:, :, h * P : (h + 1) * P],
+                )
+            for h in range(2):
+                quantize(x_op[b], h * P, (h + 1) * P)
             for q in range(chunks):
                 first_layer(b, q)
 
@@ -170,20 +176,27 @@ def tile_picked_shuffle_mlp_gelu_perm_l_kernel(tc, xT, w1, w2, offs, out):
         quantize(w2_op[1], 0, N)
         quantize(h_op[0][1], 0, PAIR)
         quantize(h_op[1][0], 0, PAIR)
-        quantize(h_op[1][1], 0, PAIR)
+        for h in range(2):
+            quantize(h_op[1][1], h * P, (h + 1) * P)
         sums0 = psum.tile([P, N // P, PAIR], F32, name="bank5")
         for m in range(N // P):
             for g in range(passes):
                 multiply(sums0[:, m, :], w2_op[g], m * P, h_op[0][g], 0, PAIR, g == 0, g == passes - 1)
-        sums1 = [psum.tile([P, PAIR], F32, name=f"bank{6 + m}") for m in range(N // P)]
-        for g in range(passes):
+        sums1 = {}
+        for h in range(2):
             for m in range(N // P):
-                multiply(sums1[m][:], w2_op[g], m * P, h_op[1][g], 0, PAIR, g == 0, g == passes - 1)
+                sums1[h, m] = psum.tile([P, P], F32, name=f"bank{(6, 7, 1, 2)[2 * h + m]}")
+        for g in range(passes):
+            for h in range(2):
+                for m in range(N // P):
+                    multiply(sums1[h, m][:], w2_op[g], m * P, h_op[1][g], h * P, P, g == 0, g == passes - 1)
         result0 = keep.tile([P, N // P, PAIR], F32, name="result0")
         nc.scalar.copy(out=result0[:], in_=sums0[:])
         nc.sync.dma_start(out=out.rearrange("(m p) t -> p m t", p=P)[:, :, :PAIR], in_=result0[:])
+        result1 = [keep.tile([P, PAIR], F32, name=f"result1_{m}") for m in range(N // P)]
+        for h in range(2):
+            for m in range(N // P):
+                copy = nc.scalar.copy if m else nc.vector.tensor_copy
+                copy(out=result1[m][:, h * P : (h + 1) * P], in_=sums1[h, m][:])
         for m in range(N // P):
-            result = keep.tile([P, PAIR], F32, name=f"result1_{m}")
-            copy = nc.scalar.copy if m else nc.vector.tensor_copy
-            copy(out=result[:], in_=sums1[m][:])
-            nc.sync.dma_start(out=out[m * P : (m + 1) * P, PAIR:], in_=result[:])
+            nc.sync.dma_start(out=out[m * P : (m + 1) * P, PAIR:], in_=result1[m][:])

from contextlib import ExitStack

import concourse.mybir as mybir
from concourse.masks import make_identity

K, T, H, N = 512, 512, 1024, 256
FLOPS = 2 * K * H * T + 2 * H * N * T

F32 = mybir.dt.float32
BF16 = mybir.dt.bfloat16
U32 = mybir.dt.uint32
U16 = mybir.dt.uint16
U8 = mybir.dt.uint8
FP8X4 = mybir.dt.float8_e4m3fn_x4
GELU = mybir.ActivationFunctionType.Gelu_apprx_tanh
MULT, ADD = mybir.AluOpType.mult, mybir.AluOpType.add

P = 128
PACK = 4
PAIR = 2 * P
CHUNK = 256
PASS = P * PACK


def tile_picked_shuffle_mlp_gelu_perm_l_kernel(tc, xT, w1, w2, offs, out):
    nc = tc.nc
    with ExitStack() as ctx:
        keep = ctx.enter_context(tc.tile_pool(name="keep", bufs=1))
        psum = ctx.enter_context(tc.psum_pool(name="psum", bufs=1))

        pairs = T // PAIR
        chunks = H // CHUNK
        passes = H // PASS

        x_rows = xT.rearrange("(p j) t -> p j t", j=PACK)
        w1_rows = w1.rearrange("(p j) c -> p j c", j=PACK)
        w2_rows = w2.rearrange("(g p j) m -> g p j m", g=passes, j=PACK)

        x_raw = [keep.tile([P, PACK, PAIR], F32, name=f"x_raw{b}") for b in range(pairs)]
        w2_raw = [keep.tile([P, PACK, N], F32, name=f"w2_raw{g}") for g in range(passes)]
        offsets = keep.tile([P, H // 16], U16, name="offsets")

        nc.sync.dma_start(out=x_raw[0][:], in_=x_rows[:, :, 0:PAIR])
        w1_raw = []
        for width in (2 * CHUNK, CHUNK, CHUNK):
            first = CHUNK * len(w1_raw)
            part = keep.tile([P, PACK, width], F32, name=f"w1_raw{first}")
            nc.sync.dma_start(out=part[:], in_=w1_rows[:, :, first : first + width])
            w1_raw += [part[:, :, s : s + CHUNK] for s in range(0, width, CHUNK)]
        for b in range(1, pairs):
            nc.sync.dma_start(out=x_raw[b][:], in_=x_rows[:, :, b * PAIR : (b + 1) * PAIR])
        nc.sync.dma_start(offsets[:], offs)
        for g in range(passes):
            nc.sync.dma_start(out=w2_raw[g][:], in_=w2_rows[g])

        ident = keep.tile([P, P], BF16, name="ident")
        make_identity(nc, ident[:])
        ident_words = keep.tile([P, P], F32, name="ident_words")
        make_identity(nc, ident_words[:])
        warm_in = keep.tile([P, 1], F32, name="warm_in")
        warm_out = keep.tile([P, 1], F32, name="warm_out")
        nc.vector.memset(warm_in[:], 0.0)
        nc.scalar.activation(warm_out[:], warm_in[:], GELU)

        def interleave(engine_copy, grouped, raw):
            engine_copy(out=grouped.rearrange("p (c j) -> p c j", j=PACK), in_=raw.rearrange("p j c -> p c j"))

        def operand(width, name, tag=None):
            grouped = keep.tile([P, PACK * width], BF16, name=name + "_grouped", tag=tag or name + "_grouped", align_bytes=64)
            codes = keep.tile([P, width], U32, name=name + "_codes", align_bytes=64)
            scales = keep.tile([P, width], U8, name=name + "_scales", align_bytes=64)
            return grouped, codes, scales

        def quantize(op, lo, hi):
            grouped, codes, scales = op
            nc.vector.quantize_mx(
                out=codes[:, lo:hi].bitcast(FP8X4), scales=scales[:, lo:hi], in_=grouped[:, PACK * lo : PACK * hi]
            )

        def multiply(bank, left, l0, right, r0, width, start, stop):
            nc.tensor.matmul_mx(
                out=bank,
                lhsT=left[1][:, l0 : l0 + P].bitcast(FP8X4),
                lhsT_scale=left[2][:, l0 : l0 + P],
                rhs=right[1][:, r0 : r0 + width].bitcast(FP8X4),
                rhs_scale=right[2][:, r0 : r0 + width],
                start=start,
                stop=stop,
            )

        x_op = [operand(PAIR, f"x{b}") for b in range(pairs)]
        w1_op = [operand(CHUNK, f"w1_{q}") for q in range(chunks)]
        window = [keep.tile([P, 2 * H], BF16, name=f"window{b}", align_bytes=64) for b in range(pairs)]

        def first_layer(b, q):
            bank = psum.tile([P, 2, CHUNK], F32, name=f"bank{4 * b + q}")
            for h in range(2):
                multiply(bank[:, h, :], x_op[b], h * P, w1_op[q], 0, CHUNK, True, True)
            nc.scalar.activation(
                window[b][:, 2 * q * CHUNK : 2 * (q + 1) * CHUNK].rearrange("p (c h) -> p c h", h=2),
                bank[:].rearrange("p h c -> p c h"),
                GELU,
            )

        interleave(nc.vector.tensor_copy, x_op[0][0][:], x_raw[0][:])
        quantize(x_op[0], 0, PAIR)
        for q in range(chunks):
            half = CHUNK // 2
            for s in range(2):
                interleave(
                    nc.scalar.copy if (q, s) == (1, 1) else nc.vector.tensor_copy,
                    w1_op[q][0][:, PACK * s * half : PACK * (s + 1) * half],
                    w1_raw[q][:, :, s * half : (s + 1) * half],
                )
            for s in range(2):
                quantize(w1_op[q], s * half, (s + 1) * half)
            first_layer(0, q)
        for b in range(1, pairs):
            for h in range(2):
                interleave(
                    nc.vector.tensor_copy,
                    x_op[b][0][:, PACK * h * P : PACK * (h + 1) * P],
                    x_raw[b][:, :, h * P : (h + 1) * P],
                )
            for h in range(2):
                quantize(x_op[b], h * P, (h + 1) * P)
            for q in range(chunks):
                first_layer(b, q)

        w2_op = [operand(N, "w2_0", "x1_grouped"), operand(N, "w2_1")]
        for g in range(passes):
            nc.gpsimd.tensor_scalar(
                out=w2_op[g][0][:].rearrange("p (c j) -> p c j", j=PACK),
                in0=w2_raw[g][:].rearrange("p j c -> p c j"),
                scalar1=1.0, scalar2=0.0, op0=MULT, op1=ADD,
            )

        h_op = [[operand(PAIR, f"h{b}_{g}") for g in range(passes)] for b in range(pairs)]
        picked = {}
        for b in range(pairs):
            for g in range(passes):
                picked[b, g] = keep.tile([P, 2 * PASS], BF16, name=f"picked{b}_{g}", align_bytes=64)
                cols = PASS // 16
                nc.vector.tensor_copy(
                    picked[b, g][:].bitcast(U32).rearrange("p (e q) -> p q e", e=PACK),
                    window[b][:].bitcast(U32).indirect(offsets[:, g * cols : (g + 1) * cols]),
                )

        def turn(b, g, name):
            words = picked[b, g][:].bitcast(F32).rearrange("p (e q) -> p e q", e=PACK)
            turned = psum.tile([P, PACK, P], F32, name=name)
            for e in range(PACK):
                nc.tensor.transpose(turned[:, e, :], words[:, e, :], ident_words[:])
            nc.scalar.copy(
                out=h_op[b][g][0][:].rearrange("p (h t e) -> p h t e", h=2, e=PACK),
                in_=turned[:].rearrange("p e t -> p (e t)").bitcast(BF16).rearrange("p (e t h) -> p h t e", e=PACK, h=2),
            )

        def turn_half(b, g, h, copy, name):
            values = picked[b, g][:].rearrange("p (e q h) -> p h e q", e=PACK, h=2)
            turned = psum.tile([P, PACK, P], BF16, name=name)
            for e in range(PACK):
                nc.tensor.transpose(turned[:, e, :], values[:, h, e, :], ident[:])
            copy(
                out=h_op[b][g][0][:, h * PASS : (h + 1) * PASS].rearrange("p (t e) -> p t e", e=PACK),
                in_=turned[:].rearrange("p e t -> p t e"),
            )

        turn(0, 0, "bank0")
        turn(0, 1, "bank1")
        turn(1, 0, "bank2")
        turn_half(1, 1, 0, nc.vector.tensor_copy, "bank3")
        turn_half(1, 1, 1, nc.scalar.copy, "bank4")
        quantize(w2_op[0], 0, N)
        quantize(h_op[0][0], 0, PAIR)
        quantize(w2_op[1], 0, N)
        quantize(h_op[0][1], 0, PAIR)
        quantize(h_op[1][0], 0, PAIR)
        for h in range(2):
            quantize(h_op[1][1], h * P, (h + 1) * P)
        sums0 = psum.tile([P, N // P, PAIR], F32, name="bank5")
        for m in range(N // P):
            for g in range(passes):
                multiply(sums0[:, m, :], w2_op[g], m * P, h_op[0][g], 0, PAIR, g == 0, g == passes - 1)
        sums1 = {}
        for h in range(2):
            for m in range(N // P):
                sums1[h, m] = psum.tile([P, P], F32, name=f"bank{(6, 7, 1, 2)[2 * h + m]}")
        for g in range(passes):
            for h in range(2):
                for m in range(N // P):
                    multiply(sums1[h, m][:], w2_op[g], m * P, h_op[1][g], h * P, P, g == 0, g == passes - 1)
        result0 = keep.tile([P, N // P, PAIR], F32, name="result0")
        nc.scalar.copy(out=result0[:], in_=sums0[:])
        nc.sync.dma_start(out=out.rearrange("(m p) t -> p m t", p=P)[:, :, :PAIR], in_=result0[:])
        result1 = [keep.tile([P, PAIR], F32, name=f"result1_{m}") for m in range(N // P)]
        for h in range(2):
            for m in range(N // P):
                copy = nc.scalar.copy if m else nc.vector.tensor_copy
                copy(out=result1[m][:, h * P : (h + 1) * P], in_=sums1[h, m][:])
        for m in range(N // P):
            nc.sync.dma_start(out=out[m * P : (m + 1) * P, PAIR:], in_=result1[m][:])
